import numpy as np
import ml_dtypes


def mxq(x, axis, fmt="e4m3"):
    dtype, down = {"e4m3": (ml_dtypes.float8_e4m3fn, 7), "e5m2": (ml_dtypes.float8_e5m2, 14)}[fmt]
    v = np.moveaxis(np.asarray(x, np.float32).astype(ml_dtypes.bfloat16).astype(np.float64), axis, -1)
    blocks = v.reshape(v.shape[:-1] + (-1, 32))
    amax = np.abs(blocks).max(-1, keepdims=True)
    byte = np.maximum(np.where(amax > 0, np.frexp(amax)[1] - 1 + 127, 0) - down, 1)
    scale = np.exp2(byte - 127.0)
    codes = (blocks / scale).astype(np.float32).astype(dtype).astype(np.float64)
    return np.moveaxis((codes * scale).reshape(v.shape), -1, axis)


WIDE = False


def mx_kscale(k):
    if not WIDE:
        return np.ones(k)
    levels = np.array([10, -10, 5, -5, 0])
    if k % 512:
        return np.exp2(np.random.permutation(np.resize(levels, k // 32))).repeat(32)
    a = np.empty((k // 512, 16))
    for p in range(k // 512):
        a[p, :8] = np.random.permutation(np.resize(levels, 8))
        for g in range(8):
            far = levels[np.abs(levels - a[p, g]) >= 10]
            a[p, g + 8] = far[np.random.randint(len(far))]
    return np.exp2(a.ravel()).repeat(32)


def f64(x):
    return np.asarray(x).astype(np.float64)


def striped(idx):
    return np.tile(idx.reshape(-1, 16).T, (8, 1)).astype(np.uint16)


def unstriped(offs):
    return offs[:16].T.reshape(-1).astype(np.int64)


def pack_weight(w):
    k, n = w.shape
    w = f64(np.asarray(w, np.float32).astype(ml_dtypes.bfloat16)).reshape(k // 32, 32, n)
    amax = np.abs(w).max(1)
    byte = np.clip(np.where(amax > 0, np.frexp(amax)[1] - 1 + 127 - 7, 1), 1, 254)
    scaled = (w * np.exp2(127.0 - byte)[:, None, :]).reshape(k, n).astype(np.float32)
    words = np.ascontiguousarray(scaled.reshape(k // 512, 128, 4, n).transpose(0, 1, 3, 2)).astype(ml_dtypes.float8_e4m3fn).view(np.uint8)
    return words, np.ascontiguousarray(byte.astype(np.uint8).reshape(k // 512, 16, n))


def unpack_weight(words, scales):
    g, p, n, _ = words.shape
    vals = np.ascontiguousarray(words).view(ml_dtypes.float8_e4m3fn).astype(np.float64) * np.repeat(np.exp2(scales.astype(np.float64) - 127.0), 8, axis=1)[..., None]
    return vals.transpose(0, 1, 3, 2).reshape(g * 512, n)


def relu(v):
    return np.maximum(v, 0.0)


K, T, D, S, V, N = 1024, 2048, 4, 512, 256, 128


def setup_inputs():
    n = np.random.standard_normal
    s = mx_kscale(K)[:, None]
    words, scales = pack_weight(n((K, N)) / np.sqrt(K) / s)
    return {
        "xT": (n((K, T)) * s).astype(np.float32),
        "w_words": words,
        "w_scales": scales,
        "b": (0.3 * n((N, 1))).astype(np.float32),
        "gate": np.tile(np.random.uniform(0.2, 1.0, (D, 1, V)) / np.sqrt(D), (1, N, 1)).astype(np.float32),
        "offs": striped(np.random.permutation(T)[:S]),
        "pos1": striped(np.random.permutation(S)[:V]),
        "pos2": striped(np.random.permutation(S)[:V]),
        "pos3": striped(np.random.permutation(S)[:V]),
        "pos4": striped(np.random.permutation(S)[:V]),
    }


def reference(xT, w_words, w_scales, b, gate, offs, pos1, pos2, pos3, pos4):
    w = unpack_weight(w_words, w_scales)
    idx = unstriped(offs)
    xq = mxq(f64(xT)[:, idx], 0, "e4m3")
    y = w.T @ xq
    y = relu(y + f64(b))
    return sum(f64(gate[d]) * y[:, unstriped(p)] for d, p in enumerate((pos1, pos2, pos3, pos4)))

@@ -1,0 +1,137 @@
+from contextlib import ExitStack
+
+import concourse.mybir as mybir
+
+K, T, D, S, V, N = 1024, 2048, 4, 512, 256, 128
+FLOPS = 2 * K * N * S
+
+F32 = mybir.dt.float32
+BF16 = mybir.dt.bfloat16
+I32 = mybir.dt.int32
+U32 = mybir.dt.uint32
+U16 = mybir.dt.uint16
+U8 = mybir.dt.uint8
+FP8X4 = mybir.dt.float8_e4m3fn_x4
+ADD = mybir.AluOpType.add
+MULT = mybir.AluOpType.mult
+MAX = mybir.AluOpType.max
+RELU = mybir.ActivationFunctionType.Relu
+
+P = 128
+PACK = 4
+K_PASS = P * PACK
+PASSES = K // K_PASS
+PER_COLUMN = 16
+PIECE = 128
+PIECES = S // PIECE
+
+
+def tile_picked_sub_lin_relu_sub_e_kernel(
+    tc, xT, w_words, w_scales, b, gate, offs, pos1, pos2, pos3, pos4, out
+):
+    nc = tc.nc
+    with ExitStack() as ctx:
+        lists = ctx.enter_context(tc.tile_pool(name="lists", bufs=1))
+        keep = ctx.enter_context(tc.tile_pool(name="keep", bufs=1))
+        psum = ctx.enter_context(tc.psum_pool(name="psum", bufs=1))
+
+        offs_sb = lists.tile([P, S // PER_COLUMN], U16, name="offs_sb")
+        pos_sb = [lists.tile([P, V // PER_COLUMN], U16, name=f"pos_sb{d}") for d in range(D)]
+
+        w_codes = keep.tile([P, PASSES, N], U32, name="w_codes", align_bytes=64)
+        w_bytes = keep.tile([P, PASSES, N], U8, name="w_bytes", align_bytes=64)
+        bias = keep.tile([P, 1], F32, name="bias")
+        gate_sb = keep.tile([P, D, V], F32, name="gate_sb")
+        warm_in = keep.tile([P, 1], F32, name="warm_in")
+        warm_out = keep.tile([P, 1], F32, name="warm_out")
+
+        nc.vector.memset(w_bytes[:].bitcast(I32), 0)
+        nc.vector.memset(warm_in[:], 0.0)
+        nc.scalar.activation(warm_out[:], warm_in[:], RELU)
+
+        rows = [keep.tile([P, T], F32, name=f"rows{i}") for i in range(PASSES * PACK)]
+        x_view = xT.rearrange("(a p t) w -> a t p w", a=PASSES, t=PACK)
+        for i in range(PASSES * PACK):
+            nc.sync.dma_start(rows[i][:], x_view[i // PACK, i % PACK])
+            if i == 0:
+                nc.sync.dma_start(offs_sb[:], offs)
+        nc.sync.dma_start(w_codes[:].bitcast(I32), w_words.rearrange("a p m r -> p a (m r)").bitcast(I32))
+        for q in range(4):
+            nc.sync.dma_start(
+                w_bytes[32 * q : 32 * q + 4].bitcast(I32),
+                w_scales[:, 4 * q : 4 * q + 4, :].rearrange("a q m -> q a m").bitcast(I32),
+            )
+        nc.sync.dma_start(bias[:], b)
+        nc.sync.dma_start(gate_sb[:], gate.rearrange("d m v -> m d v"))
+        for d, pos in enumerate((pos1, pos2, pos3, pos4)):
+            nc.sync.dma_start(pos_sb[d][:], pos)
+
+        picked = [keep.tile([P, S, PACK], BF16, name=f"picked{a}", align_bytes=64) for a in range(PASSES)]
+        x_codes = [keep.tile([P, S], U32, name=f"x_codes{a}", align_bytes=64) for a in range(PASSES)]
+        x_bytes = [keep.tile([P, S], U8, name=f"x_bytes{a}", align_bytes=64) for a in range(PASSES)]
+        acc = [psum.tile([P, 512], F32, name=f"acc{c}") for c in range(PIECES)]
+        y = keep.tile([P, S], F32, name="y")
+
+        def gather(i, lo, hi):
+            window = rows[i][:].indirect(offs_sb[:, lo // PER_COLUMN : hi // PER_COLUMN])
+            nc.vector.tensor_copy(picked[i // PACK][:, lo:hi, i % PACK], window)
+
+        def quantise(a, lo, hi):
+            nc.vector.quantize_mx(
+                out=x_codes[a][:, lo:hi].bitcast(FP8X4),
+                scales=x_bytes[a][:, lo:hi],
+                in_=picked[a][:, lo:hi, :].rearrange("p s t -> p (s t)"),
+            )
+
+        def multiply(a, c):
+            cols = slice(c * PIECE, (c + 1) * PIECE)
+            nc.tensor.matmul_mx(
+                out=acc[c][:, :PIECE],
+                lhsT=w_codes[:, a, :].bitcast(FP8X4),
+                lhsT_scale=w_bytes[:, a, :],
+                rhs=x_codes[a][:, cols].bitcast(FP8X4),
+                rhs_scale=x_bytes[a][:, cols],
+                start=(a == 0),
+                stop=(a == PASSES - 1),
+            )
+
+        for i in range(PACK):
+            gather(i, 0, S)
+        gather(PACK, 0, S)
+        quantise(0, 0, S)
+        for c in range(PIECES):
+            multiply(0, c)
+        gather(PACK + 1, 0, S)
+        gather(PACK + 2, 0, S)
+        gather(PACK + 3, 0, S // 2)
+        gather(PACK + 3, S // 2, S)
+        for c in range(PIECES):
+            quantise(1, c * PIECE, (c + 1) * PIECE)
+            multiply(1, c)
+        for c in range(PIECES):
+            cols = slice(c * PIECE, (c + 1) * PIECE)
+            if c == PIECES - 2:
+                nc.vector.tensor_scalar(y[:, cols], acc[c][:, :PIECE], bias[:], 0.0, ADD, MAX)
+            else:
+                nc.scalar.activation(y[:, cols], acc[c][:, :PIECE], RELU, bias=bias[:])
+
+        terms = [keep.tile([P, V], F32, name=f"term{d}") for d in range(D)]
+        sum01 = keep.tile([P, V], F32, name="sum01")
+        sum012 = keep.tile([P, V], F32, name="sum012")
+        total = keep.tile([P, V], F32, name="total")
+
+        def term(d, lo, hi):
+            window = y[:].indirect(pos_sb[d][:, lo // PER_COLUMN : hi // PER_COLUMN])
+            nc.vector.tensor_tensor(terms[d][:, lo:hi], window, gate_sb[:, d, lo:hi], MULT)
+
+        half = V // 2
+        term(0, 0, V)
+        term(1, 0, V)
+        term(2, 0, V)
+        nc.vector.tensor_tensor(sum01[:], terms[0][:], terms[1][:], ADD)
+        term(3, 0, half)
+        nc.vector.tensor_tensor(sum012[:], sum01[:], terms[2][:], ADD)
+        term(3, half, V)
+        for lo in (0, half):
+            nc.vector.tensor_tensor(total[:, lo : lo + half], sum012[:, lo : lo + half], terms[3][:, lo : lo + half], ADD)
+        nc.sync.dma_start(out, total[:])

@@ -15,6 +15,7 @@ FP8X4 = mybir.dt.float8_e4m3fn_x4
 ADD = mybir.AluOpType.add
 MULT = mybir.AluOpType.mult
 MAX = mybir.AluOpType.max
+COPY = mybir.ActivationFunctionType.Copy
 RELU = mybir.ActivationFunctionType.Relu
 
 P = 128
@@ -24,6 +25,9 @@ PASSES = K // K_PASS
 PER_COLUMN = 16
 PIECE = 128
 PIECES = S // PIECE
+LAST = PASSES * PACK - 1
+CUT = 1536
+CASTS = ((0, 1024, "vector"), (1024, 1536, "scalar"), (1536, 1856, "vector"), (1856, 2048, "scalar"))
 
 
 def tile_picked_sub_lin_relu_sub_e_kernel(
@@ -52,7 +56,11 @@ def tile_picked_sub_lin_relu_sub_e_kernel(
         rows = [keep.tile([P, T], F32, name=f"rows{i}") for i in range(PASSES * PACK)]
         x_view = xT.rearrange("(a p t) w -> a t p w", a=PASSES, t=PACK)
         for i in range(PASSES * PACK):
-            nc.sync.dma_start(rows[i][:], x_view[i // PACK, i % PACK])
+            if i == LAST:
+                nc.sync.dma_start(rows[i][:, :CUT], x_view[i // PACK, i % PACK, :, :CUT])
+                nc.sync.dma_start(rows[i][:, CUT:], x_view[i // PACK, i % PACK, :, CUT:])
+            else:
+                nc.sync.dma_start(rows[i][:], x_view[i // PACK, i % PACK])
             if i == 0:
                 nc.sync.dma_start(offs_sb[:], offs)
         nc.sync.dma_start(w_codes[:].bitcast(I32), w_words.rearrange("a p m r -> p a (m r)").bitcast(I32))
@@ -103,8 +111,18 @@ def tile_picked_sub_lin_relu_sub_e_kernel(
             multiply(0, c)
         gather(PACK + 1, 0, S)
         gather(PACK + 2, 0, S)
-        gather(PACK + 3, 0, S // 2)
-        gather(PACK + 3, S // 2, S)
+        last_bf16 = keep.tile([P, T], BF16, name="last_bf16")
+        for lo, hi, engine in CASTS:
+            if engine == "vector":
+                nc.vector.tensor_copy(last_bf16[:, lo:hi], rows[LAST][:, lo:hi])
+            else:
+                nc.scalar.copy(last_bf16[:, lo:hi], rows[LAST][:, lo:hi])
+        gather(LAST, 0, S // 2)
+        nc.scalar.activation(
+            picked[1][:, S // 2 :, PACK - 1],
+            last_bf16[:].indirect(offs_sb[:, S // 2 // PER_COLUMN :]),
+            COPY,
+        )
         for c in range(PIECES):
             quantise(1, c * PIECE, (c + 1) * PIECE)
             multiply(1, c)

@@ -1,6 +1,7 @@
 from contextlib import ExitStack
 
 import concourse.mybir as mybir
+from concourse.masks import make_identity
 
 K, T, D, S, V, N = 1024, 2048, 4, 512, 256, 128
 FLOPS = 2 * K * N * S
@@ -45,13 +46,16 @@ def tile_picked_sub_lin_relu_sub_e_kernel(
         w_codes = keep.tile([P, PASSES, N], U32, name="w_codes", align_bytes=64)
         w_bytes = keep.tile([P, PASSES, N], U8, name="w_bytes", align_bytes=64)
         bias = keep.tile([P, 1], F32, name="bias")
-        gate_sb = keep.tile([P, D, V], F32, name="gate_sb")
+        gate_cols = keep.tile([P, 4], F32, name="gate_cols")
+        gate_sb = keep.tile([P, 2, V], F32, name="gate_sb")
+        ident = keep.tile([P, P], F32, name="ident")
         warm_in = keep.tile([P, 1], F32, name="warm_in")
         warm_out = keep.tile([P, 1], F32, name="warm_out")
 
         nc.vector.memset(w_bytes[:].bitcast(I32), 0)
         nc.vector.memset(warm_in[:], 0.0)
         nc.scalar.activation(warm_out[:], warm_in[:], RELU)
+        make_identity(nc, ident[:])
 
         rows = [keep.tile([P, T], F32, name=f"rows{i}") for i in range(PASSES * PACK)]
         x_view = xT.rearrange("(a p t) w -> a t p w", a=PASSES, t=PACK)
@@ -70,14 +74,18 @@ def tile_picked_sub_lin_relu_sub_e_kernel(
                 w_scales[:, 4 * q : 4 * q + 4, :].rearrange("a q m -> q a m").bitcast(I32),
             )
         nc.sync.dma_start(bias[:], b)
-        nc.sync.dma_start(gate_sb[:], gate.rearrange("d m v -> m d v"))
-        for d, pos in enumerate((pos1, pos2, pos3, pos4)):
-            nc.sync.dma_start(pos_sb[d][:], pos)
+        nc.sync.dma_start(pos_sb[0][:], pos1)
+        nc.sync.dma_start(pos_sb[1][:], pos2)
+        with nc.allow_non_contiguous_dma(reason="one gate weight a partition"):
+            nc.sync.dma_start(gate_cols[:], gate.rearrange("d m (h p) -> (d m h) p", h=2)[0 : 4 * (P + 1) : P + 1].rearrange("j p -> p j"))
+        nc.sync.dma_start(gate_sb[:], gate[2:4].rearrange("d m v -> m d v"))
+        nc.sync.dma_start(pos_sb[2][:], pos3)
+        nc.sync.dma_start(pos_sb[3][:], pos4)
 
         picked = [keep.tile([P, S, PACK], BF16, name=f"picked{a}", align_bytes=64) for a in range(PASSES)]
         x_codes = [keep.tile([P, S], U32, name=f"x_codes{a}", align_bytes=64) for a in range(PASSES)]
         x_bytes = [keep.tile([P, S], U8, name=f"x_bytes{a}", align_bytes=64) for a in range(PASSES)]
-        acc = [psum.tile([P, 512], F32, name=f"acc{c}") for c in range(PIECES)]
+        acc = [psum.tile([P, 512], F32, name=f"acc{c}", tag=f"bank{c}") for c in range(PIECES)]
         y = keep.tile([P, S], F32, name="y")
 
         def gather(i, lo, hi):
@@ -133,23 +141,37 @@ def tile_picked_sub_lin_relu_sub_e_kernel(
             else:
                 nc.scalar.activation(y[:, cols], acc[c][:, :PIECE], RELU, bias=bias[:])
 
-        terms = [keep.tile([P, V], F32, name=f"term{d}") for d in range(D)]
-        sum01 = keep.tile([P, V], F32, name="sum01")
-        sum012 = keep.tile([P, V], F32, name="sum012")
+        def places(d):
+            return y[:].indirect(pos_sb[d][:])
+
+        plain = [keep.tile([P, V], F32, name=f"plain{d}") for d in range(2)]
+        fused = [keep.tile([P, V], F32, name=f"fused{d}") for d in range(2)]
+        for d in range(2):
+            nc.vector.tensor_copy(plain[d][:], places(d))
+        for d in range(2):
+            nc.vector.tensor_tensor(fused[d][:], places(2 + d), gate_sb[:, d, :], MULT)
+
+        sums = [psum.tile([P, 512], F32, name=f"sum{h}", tag=f"side{h}") for h in range(2)]
+        scaled = {}
+        for d in range(2):
+            for h in range(2):
+                flipped = psum.tile([P, 512], F32, name=f"flipped{d}{h}", tag=f"bank{2 * d + h}")
+                nc.tensor.transpose(flipped[:, :P], plain[d][:, h * P : (h + 1) * P], ident[:])
+                weighted = keep.tile([P, P], F32, name=f"weighted{d}{h}")
+                nc.scalar.activation(weighted[:], flipped[:, :P], COPY, scale=gate_cols[:, 2 * d + h : 2 * d + h + 1])
+                scaled[d, h] = weighted
+        for d in range(2):
+            for h in range(2):
+                nc.tensor.matmul(
+                    sums[h][:, :P], scaled[d, h][:], ident[:], start=(d == 0), stop=(d == 1), is_transpose=True
+                )
+
+        pair = keep.tile([P, V], F32, name="pair")
         total = keep.tile([P, V], F32, name="total")
-
-        def term(d, lo, hi):
-            window = y[:].indirect(pos_sb[d][:, lo // PER_COLUMN : hi // PER_COLUMN])
-            nc.vector.tensor_tensor(terms[d][:, lo:hi], window, gate_sb[:, d, lo:hi], MULT)
-
-        half = V // 2
-        term(0, 0, V)
-        term(1, 0, V)
-        term(2, 0, V)
-        nc.vector.tensor_tensor(sum01[:], terms[0][:], terms[1][:], ADD)
-        term(3, 0, half)
-        nc.vector.tensor_tensor(sum012[:], sum01[:], terms[2][:], ADD)
-        term(3, half, V)
-        for lo in (0, half):
-            nc.vector.tensor_tensor(total[:, lo : lo + half], sum012[:, lo : lo + half], terms[3][:, lo : lo + half], ADD)
+        for h in range(2):
+            cols = slice(h * P, (h + 1) * P)
+            nc.vector.tensor_tensor(pair[:, cols], fused[0][:, cols], fused[1][:, cols], ADD)
+        for h in range(2):
+            cols = slice(h * P, (h + 1) * P)
+            nc.vector.tensor_tensor(total[:, cols], sums[h][:, :P], pair[:, cols], ADD)
         nc.sync.dma_start(out, total[:])

@@ -148,8 +148,11 @@ def tile_picked_sub_lin_relu_sub_e_kernel(
         fused = [keep.tile([P, V], F32, name=f"fused{d}") for d in range(2)]
         for d in range(2):
             nc.vector.tensor_copy(plain[d][:], places(d))
-        for d in range(2):
-            nc.vector.tensor_tensor(fused[d][:], places(2 + d), gate_sb[:, d, :], MULT)
+        nc.vector.tensor_tensor(fused[0][:], places(2), gate_sb[:, 0, :], MULT)
+        for h in range(2):
+            cols = slice(h * P, (h + 1) * P)
+            window = y[:].indirect(pos_sb[3][:, h * P // PER_COLUMN : (h + 1) * P // PER_COLUMN])
+            nc.vector.tensor_tensor(fused[1][:, cols], window, gate_sb[:, 1, cols], MULT)
 
         sums = [psum.tile([P, 512], F32, name=f"sum{h}", tag=f"side{h}") for h in range(2)]
         scaled = {}
@@ -174,4 +177,4 @@ def tile_picked_sub_lin_relu_sub_e_kernel(
         for h in range(2):
             cols = slice(h * P, (h + 1) * P)
             nc.vector.tensor_tensor(total[:, cols], sums[h][:, :P], pair[:, cols], ADD)
-        nc.sync.dma_start(out, total[:])
+            nc.sync.dma_start(out[:, cols], total[:, cols])

@@ -21,14 +21,18 @@ RELU = mybir.ActivationFunctionType.Relu
 
 P = 128
 PACK = 4
-K_PASS = P * PACK
-PASSES = K // K_PASS
+PASSES = K // (P * PACK)
+PLANES = PASSES * PACK
+LAST = PLANES - 1
 PER_COLUMN = 16
+BANK = 512
+BURST = 256
 PIECE = 128
 PIECES = S // PIECE
-LAST = PASSES * PACK - 1
+HALF = S // 2
 CUT = 1536
-CASTS = ((0, 1024, "vector"), (1024, 1536, "scalar"), (1536, 1856, "vector"), (1856, 2048, "scalar"))
+CASTS = ((0, 1024, "vector"), (1024, CUT, "scalar"), (CUT, 1856, "vector"), (1856, T, "scalar"))
+TURNED = 2
 
 
 def tile_picked_sub_lin_relu_sub_e_kernel(
@@ -43,11 +47,14 @@ def tile_picked_sub_lin_relu_sub_e_kernel(
         offs_sb = lists.tile([P, S // PER_COLUMN], U16, name="offs_sb")
         pos_sb = [lists.tile([P, V // PER_COLUMN], U16, name=f"pos_sb{d}") for d in range(D)]
 
-        w_codes = keep.tile([P, PASSES, N], U32, name="w_codes", align_bytes=64)
+        def entries(list_sb, lo, hi):
+            return list_sb[:, lo // PER_COLUMN : hi // PER_COLUMN]
+
+        w_codes = keep.tile([P, PASSES, N], U32, name="w_codes", align_bytes=BURST)
         w_bytes = keep.tile([P, PASSES, N], U8, name="w_bytes", align_bytes=64)
         bias = keep.tile([P, 1], F32, name="bias")
-        gate_cols = keep.tile([P, 4], F32, name="gate_cols")
-        gate_sb = keep.tile([P, 2, V], F32, name="gate_sb")
+        gate_cols = keep.tile([P, 2 * TURNED], F32, name="gate_cols")
+        gate_rows = keep.tile([P, D - TURNED, V], F32, name="gate_rows", align_bytes=BURST)
         ident = keep.tile([P, P], F32, name="ident")
         warm_in = keep.tile([P, 1], F32, name="warm_in")
         warm_out = keep.tile([P, 1], F32, name="warm_out")
@@ -57,16 +64,15 @@ def tile_picked_sub_lin_relu_sub_e_kernel(
         nc.scalar.activation(warm_out[:], warm_in[:], RELU)
         make_identity(nc, ident[:])
 
-        rows = [keep.tile([P, T], F32, name=f"rows{i}") for i in range(PASSES * PACK)]
+        planes = [keep.tile([P, T], F32, name=f"plane{i}", align_bytes=BURST) for i in range(PLANES)]
         x_view = xT.rearrange("(a p t) w -> a t p w", a=PASSES, t=PACK)
-        for i in range(PASSES * PACK):
-            if i == LAST:
-                nc.sync.dma_start(rows[i][:, :CUT], x_view[i // PACK, i % PACK, :, :CUT])
-                nc.sync.dma_start(rows[i][:, CUT:], x_view[i // PACK, i % PACK, :, CUT:])
-            else:
-                nc.sync.dma_start(rows[i][:], x_view[i // PACK, i % PACK])
+        for i in range(LAST):
+            nc.sync.dma_start(planes[i][:], x_view[i // PACK, i % PACK])
             if i == 0:
                 nc.sync.dma_start(offs_sb[:], offs)
+        last_view = x_view[PASSES - 1, PACK - 1]
+        nc.sync.dma_start(planes[LAST][:, :CUT], last_view[:, :CUT])
+        nc.sync.dma_start(planes[LAST][:, CUT:], last_view[:, CUT:])
         nc.sync.dma_start(w_codes[:].bitcast(I32), w_words.rearrange("a p m r -> p a (m r)").bitcast(I32))
         for q in range(4):
             nc.sync.dma_start(
@@ -76,20 +82,21 @@ def tile_picked_sub_lin_relu_sub_e_kernel(
         nc.sync.dma_start(bias[:], b)
         nc.sync.dma_start(pos_sb[0][:], pos1)
         nc.sync.dma_start(pos_sb[1][:], pos2)
+        half_rows = gate.rearrange("d m (h p) -> (d m h) p", h=2)
         with nc.allow_non_contiguous_dma(reason="one gate weight a partition"):
-            nc.sync.dma_start(gate_cols[:], gate.rearrange("d m (h p) -> (d m h) p", h=2)[0 : 4 * (P + 1) : P + 1].rearrange("j p -> p j"))
-        nc.sync.dma_start(gate_sb[:], gate[2:4].rearrange("d m v -> m d v"))
+            nc.sync.dma_start(gate_cols[:], half_rows[0 : 2 * TURNED * (N + 1) : N + 1].rearrange("j p -> p j"))
+        nc.sync.dma_start(gate_rows[:], gate[TURNED:].rearrange("d m v -> m d v"))
         nc.sync.dma_start(pos_sb[2][:], pos3)
         nc.sync.dma_start(pos_sb[3][:], pos4)
 
         picked = [keep.tile([P, S, PACK], BF16, name=f"picked{a}", align_bytes=64) for a in range(PASSES)]
         x_codes = [keep.tile([P, S], U32, name=f"x_codes{a}", align_bytes=64) for a in range(PASSES)]
         x_bytes = [keep.tile([P, S], U8, name=f"x_bytes{a}", align_bytes=64) for a in range(PASSES)]
-        acc = [psum.tile([P, 512], F32, name=f"acc{c}", tag=f"bank{c}") for c in range(PIECES)]
+        acc = [psum.tile([P, BANK], F32, name=f"acc{c}", tag=f"bank{c}") for c in range(PIECES)]
         y = keep.tile([P, S], F32, name="y")
 
-        def gather(i, lo, hi):
-            window = rows[i][:].indirect(offs_sb[:, lo // PER_COLUMN : hi // PER_COLUMN])
+        def gather_into_slot(i, lo, hi):
+            window = planes[i][:].indirect(entries(offs_sb, lo, hi))
             nc.vector.tensor_copy(picked[i // PACK][:, lo:hi, i % PACK], window)
 
         def quantise(a, lo, hi):
@@ -111,29 +118,27 @@ def tile_picked_sub_lin_relu_sub_e_kernel(
                 stop=(a == PASSES - 1),
             )
 
-        for i in range(PACK):
-            gather(i, 0, S)
-        gather(PACK, 0, S)
+        for i in range(PACK + 1):
+            gather_into_slot(i, 0, S)
         quantise(0, 0, S)
         for c in range(PIECES):
             multiply(0, c)
-        gather(PACK + 1, 0, S)
-        gather(PACK + 2, 0, S)
+        for i in range(PACK + 1, LAST):
+            gather_into_slot(i, 0, S)
+
         last_bf16 = keep.tile([P, T], BF16, name="last_bf16")
         for lo, hi, engine in CASTS:
             if engine == "vector":
-                nc.vector.tensor_copy(last_bf16[:, lo:hi], rows[LAST][:, lo:hi])
+                nc.vector.tensor_copy(last_bf16[:, lo:hi], planes[LAST][:, lo:hi])
             else:
-                nc.scalar.copy(last_bf16[:, lo:hi], rows[LAST][:, lo:hi])
-        gather(LAST, 0, S // 2)
+                nc.scalar.copy(last_bf16[:, lo:hi], planes[LAST][:, lo:hi])
+        gather_into_slot(LAST, 0, HALF)
         nc.scalar.activation(
-            picked[1][:, S // 2 :, PACK - 1],
-            last_bf16[:].indirect(offs_sb[:, S // 2 // PER_COLUMN :]),
-            COPY,
+            picked[PASSES - 1][:, HALF:, PACK - 1], last_bf16[:].indirect(entries(offs_sb, HALF, S)), COPY
         )
         for c in range(PIECES):
-            quantise(1, c * PIECE, (c + 1) * PIECE)
-            multiply(1, c)
+            quantise(PASSES - 1, c * PIECE, (c + 1) * PIECE)
+            multiply(PASSES - 1, c)
         for c in range(PIECES):
             cols = slice(c * PIECE, (c + 1) * PIECE)
             if c == PIECES - 2:
@@ -141,40 +146,41 @@ def tile_picked_sub_lin_relu_sub_e_kernel(
             else:
                 nc.scalar.activation(y[:, cols], acc[c][:, :PIECE], RELU, bias=bias[:])
 
-        def places(d):
-            return y[:].indirect(pos_sb[d][:])
+        halves = (slice(0, P), slice(P, V))
+        plain = [keep.tile([P, V], F32, name=f"plain{d}") for d in range(TURNED)]
+        fused = [keep.tile([P, V], F32, name=f"fused{j}") for j in range(D - TURNED)]
+        for d in range(TURNED):
+            nc.vector.tensor_copy(plain[d][:], y[:].indirect(pos_sb[d][:]))
+        nc.vector.tensor_tensor(fused[0][:], y[:].indirect(pos_sb[TURNED][:]), gate_rows[:, 0, :], MULT)
+        for cols in halves:
+            window = y[:].indirect(entries(pos_sb[TURNED + 1], cols.start, cols.stop))
+            nc.vector.tensor_tensor(fused[1][:, cols], window, gate_rows[:, 1, cols], MULT)
 
-        plain = [keep.tile([P, V], F32, name=f"plain{d}") for d in range(2)]
-        fused = [keep.tile([P, V], F32, name=f"fused{d}") for d in range(2)]
-        for d in range(2):
-            nc.vector.tensor_copy(plain[d][:], places(d))
-        nc.vector.tensor_tensor(fused[0][:], places(2), gate_sb[:, 0, :], MULT)
-        for h in range(2):
-            cols = slice(h * P, (h + 1) * P)
-            window = y[:].indirect(pos_sb[3][:, h * P // PER_COLUMN : (h + 1) * P // PER_COLUMN])
-            nc.vector.tensor_tensor(fused[1][:, cols], window, gate_sb[:, 1, cols], MULT)
-
-        sums = [psum.tile([P, 512], F32, name=f"sum{h}", tag=f"side{h}") for h in range(2)]
-        scaled = {}
-        for d in range(2):
-            for h in range(2):
-                flipped = psum.tile([P, 512], F32, name=f"flipped{d}{h}", tag=f"bank{2 * d + h}")
-                nc.tensor.transpose(flipped[:, :P], plain[d][:, h * P : (h + 1) * P], ident[:])
-                weighted = keep.tile([P, P], F32, name=f"weighted{d}{h}")
-                nc.scalar.activation(weighted[:], flipped[:, :P], COPY, scale=gate_cols[:, 2 * d + h : 2 * d + h + 1])
-                scaled[d, h] = weighted
-        for d in range(2):
+        sums = [psum.tile([P, BANK], F32, name=f"sum{h}") for h in range(2)]
+        weighted = {}
+        for d in range(TURNED):
+            for h, cols in enumerate(halves):
+                j = 2 * d + h
+                flipped = psum.tile([P, BANK], F32, name=f"flipped{j}", tag=f"bank{j}")
+                nc.tensor.transpose(flipped[:, :P], plain[d][:, cols], ident[:])
+                product = keep.tile([P, P], F32, name=f"product{j}")
+                nc.scalar.activation(product[:], flipped[:, :P], COPY, scale=gate_cols[:, j : j + 1])
+                weighted[d, h] = product
+        for d in range(TURNED):
             for h in range(2):
                 nc.tensor.matmul(
-                    sums[h][:, :P], scaled[d, h][:], ident[:], start=(d == 0), stop=(d == 1), is_transpose=True
+                    sums[h][:, :P],
+                    weighted[d, h][:],
+                    ident[:],
+                    start=(d == 0),
+                    stop=(d == TURNED - 1),
+                    is_transpose=True,
                 )
 
         pair = keep.tile([P, V], F32, name="pair")
-        total = keep.tile([P, V], F32, name="total")
-        for h in range(2):
-            cols = slice(h * P, (h + 1) * P)
+        total = keep.tile([P, V], F32, name="total", align_bytes=BURST)
+        for cols in halves:
             nc.vector.tensor_tensor(pair[:, cols], fused[0][:, cols], fused[1][:, cols], ADD)
-        for h in range(2):
-            cols = slice(h * P, (h + 1) * P)
+        for h, cols in enumerate(halves):
             nc.vector.tensor_tensor(total[:, cols], sums[h][:, :P], pair[:, cols], ADD)
             nc.sync.dma_start(out[:, cols], total[:, cols])

@@ -30,8 +30,8 @@ BURST = 256
 PIECE = 128
 PIECES = S // PIECE
 HALF = S // 2
-CUT = 1536
-CASTS = ((0, 1024, "vector"), (1024, CUT, "scalar"), (CUT, 1856, "vector"), (1856, T, "scalar"))
+CUT = 1280
+CASTS = ((0, 576, "vector"), (576, CUT, "scalar"), (CUT, 1760, "vector"), (1760, T, "scalar"))
 TURNED = 2
 
 
@@ -136,8 +136,10 @@ def tile_picked_sub_lin_relu_sub_e_kernel(
         nc.scalar.activation(
             picked[PASSES - 1][:, HALF:, PACK - 1], last_bf16[:].indirect(entries(offs_sb, HALF, S)), COPY
         )
+        quantise(PASSES - 1, 0, HALF)
         for c in range(PIECES):
-            quantise(PASSES - 1, c * PIECE, (c + 1) * PIECE)
+            if c * PIECE >= HALF:
+                quantise(PASSES - 1, c * PIECE, (c + 1) * PIECE)
             multiply(PASSES - 1, c)
         for c in range(PIECES):
             cols = slice(c * PIECE, (c + 1) * PIECE)

@@ -1,7 +1,6 @@
 from contextlib import ExitStack
 
 import concourse.mybir as mybir
-from concourse.masks import make_identity
 
 K, T, D, S, V, N = 1024, 2048, 4, 512, 256, 128
 FLOPS = 2 * K * N * S
@@ -30,9 +29,7 @@ BURST = 256
 PIECE = 128
 PIECES = S // PIECE
 HALF = S // 2
-CUT = 1280
-CASTS = ((0, 576, "vector"), (576, CUT, "scalar"), (CUT, 1760, "vector"), (1760, T, "scalar"))
-TURNED = 2
+PLAIN = 2
 
 
 def tile_picked_sub_lin_relu_sub_e_kernel(
@@ -53,26 +50,17 @@ def tile_picked_sub_lin_relu_sub_e_kernel(
         w_codes = keep.tile([P, PASSES, N], U32, name="w_codes", align_bytes=BURST)
         w_bytes = keep.tile([P, PASSES, N], U8, name="w_bytes", align_bytes=64)
         bias = keep.tile([P, 1], F32, name="bias")
-        gate_cols = keep.tile([P, 2 * TURNED], F32, name="gate_cols")
-        gate_rows = keep.tile([P, D - TURNED, V], F32, name="gate_rows", align_bytes=BURST)
-        ident = keep.tile([P, P], F32, name="ident")
-        warm_in = keep.tile([P, 1], F32, name="warm_in")
-        warm_out = keep.tile([P, 1], F32, name="warm_out")
+        gate_plain = keep.tile([P, PLAIN, V], F32, name="gate_plain", align_bytes=BURST)
+        gate_fused = keep.tile([P, D - PLAIN, V], F32, name="gate_fused", align_bytes=BURST)
 
         nc.vector.memset(w_bytes[:].bitcast(I32), 0)
-        nc.vector.memset(warm_in[:], 0.0)
-        nc.scalar.activation(warm_out[:], warm_in[:], RELU)
-        make_identity(nc, ident[:])
 
         planes = [keep.tile([P, T], F32, name=f"plane{i}", align_bytes=BURST) for i in range(PLANES)]
         x_view = xT.rearrange("(a p t) w -> a t p w", a=PASSES, t=PACK)
-        for i in range(LAST):
+        for i in range(PLANES):
             nc.sync.dma_start(planes[i][:], x_view[i // PACK, i % PACK])
             if i == 0:
                 nc.sync.dma_start(offs_sb[:], offs)
-        last_view = x_view[PASSES - 1, PACK - 1]
-        nc.sync.dma_start(planes[LAST][:, :CUT], last_view[:, :CUT])
-        nc.sync.dma_start(planes[LAST][:, CUT:], last_view[:, CUT:])
         nc.sync.dma_start(w_codes[:].bitcast(I32), w_words.rearrange("a p m r -> p a (m r)").bitcast(I32))
         for q in range(4):
             nc.sync.dma_start(
@@ -81,13 +69,11 @@ def tile_picked_sub_lin_relu_sub_e_kernel(
             )
         nc.sync.dma_start(bias[:], b)
         nc.sync.dma_start(pos_sb[0][:], pos1)
-        nc.sync.dma_start(pos_sb[1][:], pos2)
-        half_rows = gate.rearrange("d m (h p) -> (d m h) p", h=2)
-        with nc.allow_non_contiguous_dma(reason="one gate weight a partition"):
-            nc.sync.dma_start(gate_cols[:], half_rows[0 : 2 * TURNED * (N + 1) : N + 1].rearrange("j p -> p j"))
-        nc.sync.dma_start(gate_rows[:], gate[TURNED:].rearrange("d m v -> m d v"))
         nc.sync.dma_start(pos_sb[2][:], pos3)
+        nc.sync.dma_start(gate_fused[:], gate[PLAIN:].rearrange("d m v -> m d v"))
+        nc.sync.dma_start(pos_sb[1][:], pos2)
         nc.sync.dma_start(pos_sb[3][:], pos4)
+        nc.sync.dma_start(gate_plain[:], gate[:PLAIN].rearrange("d m v -> m d v"))
 
         picked = [keep.tile([P, S, PACK], BF16, name=f"picked{a}", align_bytes=64) for a in range(PASSES)]
         x_codes = [keep.tile([P, S], U32, name=f"x_codes{a}", align_bytes=64) for a in range(PASSES)]
@@ -123,66 +109,50 @@ def tile_picked_sub_lin_relu_sub_e_kernel(
         quantise(0, 0, S)
         for c in range(PIECES):
             multiply(0, c)
-        for i in range(PACK + 1, LAST):
+        for i in range(PACK + 1, LAST - 1):
             gather_into_slot(i, 0, S)
 
-        last_bf16 = keep.tile([P, T], BF16, name="last_bf16")
-        for lo, hi, engine in CASTS:
-            if engine == "vector":
-                nc.vector.tensor_copy(last_bf16[:, lo:hi], planes[LAST][:, lo:hi])
-            else:
-                nc.scalar.copy(last_bf16[:, lo:hi], planes[LAST][:, lo:hi])
+        def gather_flat(dst, i, c):
+            window = planes[i][:].indirect(entries(offs_sb, c * PIECE, (c + 1) * PIECE))
+            nc.scalar.activation(dst, window, COPY)
+
+        pair_flat = keep.tile([P, 2, PIECE], BF16, name="pair_flat")
+        flat = keep.tile([P, PIECE], BF16, name="flat")
+        gather_into_slot(LAST - 1, 0, 3 * PIECE)
+        gather_flat(pair_flat[:, 0, :], LAST - 1, 3)
+
         gather_into_slot(LAST, 0, HALF)
-        nc.scalar.activation(
-            picked[PASSES - 1][:, HALF:, PACK - 1], last_bf16[:].indirect(entries(offs_sb, HALF, S)), COPY
-        )
+        gather_flat(pair_flat[:, 1, :], LAST, 3)
+        gather_flat(flat[:], LAST, 2)
+        nc.scalar.copy(picked[PASSES - 1][:, 3 * PIECE :, 2:], pair_flat[:].rearrange("p t s -> p s t"))
+        nc.vector.tensor_copy(picked[PASSES - 1][:, 2 * PIECE : 3 * PIECE, PACK - 1], flat[:])
         quantise(PASSES - 1, 0, HALF)
-        for c in range(PIECES):
+        for c in (0, 1, 3, 2):
             if c * PIECE >= HALF:
                 quantise(PASSES - 1, c * PIECE, (c + 1) * PIECE)
             multiply(PASSES - 1, c)
-        for c in range(PIECES):
+        for c in (0, 1, 3, 2):
             cols = slice(c * PIECE, (c + 1) * PIECE)
-            if c == PIECES - 2:
+            if c == PIECES - 1:
                 nc.vector.tensor_scalar(y[:, cols], acc[c][:, :PIECE], bias[:], 0.0, ADD, MAX)
             else:
                 nc.scalar.activation(y[:, cols], acc[c][:, :PIECE], RELU, bias=bias[:])
 
         halves = (slice(0, P), slice(P, V))
-        plain = [keep.tile([P, V], F32, name=f"plain{d}") for d in range(TURNED)]
-        fused = [keep.tile([P, V], F32, name=f"fused{j}") for j in range(D - TURNED)]
-        for d in range(TURNED):
-            nc.vector.tensor_copy(plain[d][:], y[:].indirect(pos_sb[d][:]))
-        nc.vector.tensor_tensor(fused[0][:], y[:].indirect(pos_sb[TURNED][:]), gate_rows[:, 0, :], MULT)
-        for cols in halves:
-            window = y[:].indirect(entries(pos_sb[TURNED + 1], cols.start, cols.stop))
-            nc.vector.tensor_tensor(fused[1][:, cols], window, gate_rows[:, 1, cols], MULT)
-
-        sums = [psum.tile([P, BANK], F32, name=f"sum{h}") for h in range(2)]
-        weighted = {}
-        for d in range(TURNED):
-            for h, cols in enumerate(halves):
-                j = 2 * d + h
-                flipped = psum.tile([P, BANK], F32, name=f"flipped{j}", tag=f"bank{j}")
-                nc.tensor.transpose(flipped[:, :P], plain[d][:, cols], ident[:])
-                product = keep.tile([P, P], F32, name=f"product{j}")
-                nc.scalar.activation(product[:], flipped[:, :P], COPY, scale=gate_cols[:, j : j + 1])
-                weighted[d, h] = product
-        for d in range(TURNED):
-            for h in range(2):
-                nc.tensor.matmul(
-                    sums[h][:, :P],
-                    weighted[d, h][:],
-                    ident[:],
-                    start=(d == 0),
-                    stop=(d == TURNED - 1),
-                    is_transpose=True,
-                )
-
+        plain = [keep.tile([P, V], F32, name=f"plain{d}") for d in range(PLAIN)]
+        product = [keep.tile([P, V], F32, name=f"product{d}") for d in range(D)]
+        for d in range(PLAIN):
+            nc.scalar.activation(plain[d][:], y[:].indirect(pos_sb[d][:]), COPY)
+        for d in range(PLAIN, D):
+            nc.vector.tensor_tensor(product[d][:], y[:].indirect(pos_sb[d][:]), gate_fused[:, d - PLAIN, :], MULT)
         pair = keep.tile([P, V], F32, name="pair")
+        triple = keep.tile([P, V], F32, name="triple")
         total = keep.tile([P, V], F32, name="total", align_bytes=BURST)
+        nc.vector.tensor_tensor(product[0][:], plain[0][:], gate_plain[:, 0, :], MULT)
+        nc.vector.tensor_tensor(pair[:], product[2][:], product[3][:], ADD)
+        nc.vector.tensor_tensor(product[1][:], plain[1][:], gate_plain[:, 1, :], MULT)
         for cols in halves:
-            nc.vector.tensor_tensor(pair[:, cols], fused[0][:, cols], fused[1][:, cols], ADD)
-        for h, cols in enumerate(halves):
-            nc.vector.tensor_tensor(total[:, cols], sums[h][:, :P], pair[:, cols], ADD)
+            nc.vector.tensor_tensor(triple[:, cols], pair[:, cols], product[0][:, cols], ADD)
+        for cols in halves:
+            nc.vector.tensor_tensor(total[:, cols], triple[:, cols], product[1][:, cols], ADD)
             nc.sync.dma_start(out[:, cols], total[:, cols])

@@ -68,11 +68,11 @@ def tile_picked_sub_lin_relu_sub_e_kernel(
                 w_scales[:, 4 * q : 4 * q + 4, :].rearrange("a q m -> q a m").bitcast(I32),
             )
         nc.sync.dma_start(bias[:], b)
-        nc.sync.dma_start(pos_sb[0][:], pos1)
-        nc.sync.dma_start(pos_sb[2][:], pos3)
         nc.sync.dma_start(gate_fused[:], gate[PLAIN:].rearrange("d m v -> m d v"))
-        nc.sync.dma_start(pos_sb[1][:], pos2)
+        nc.sync.dma_start(pos_sb[2][:], pos3)
+        nc.sync.dma_start(pos_sb[0][:], pos1)
         nc.sync.dma_start(pos_sb[3][:], pos4)
+        nc.sync.dma_start(pos_sb[1][:], pos2)
         nc.sync.dma_start(gate_plain[:], gate[:PLAIN].rearrange("d m v -> m d v"))
 
         picked = [keep.tile([P, S, PACK], BF16, name=f"picked{a}", align_bytes=64) for a in range(PASSES)]

@@ -29,6 +29,7 @@ BURST = 256
 PIECE = 128
 PIECES = S // PIECE
 HALF = S // 2
+DIRECT = 320
 PLAIN = 2
 
 
@@ -104,28 +105,29 @@ def tile_picked_sub_lin_relu_sub_e_kernel(
                 stop=(a == PASSES - 1),
             )
 
-        for i in range(PACK + 1):
+        def gather_flat(i, lo, hi):
+            flat = keep.tile([P, hi - lo], BF16, name=f"flat{i}_{lo}")
+            nc.scalar.activation(flat[:], planes[i][:].indirect(entries(offs_sb, lo, hi)), COPY)
+            return flat
+
+        def slot(i, lo, hi):
+            return picked[i // PACK][:, lo:hi, i % PACK]
+
+        for i in range(PACK):
             gather_into_slot(i, 0, S)
-        quantise(0, 0, S)
-        for c in range(PIECES):
-            multiply(0, c)
-        for i in range(PACK + 1, LAST - 1):
-            gather_into_slot(i, 0, S)
+        for i in range(PACK, LAST):
+            gather_into_slot(i, 0, S - PIECE)
+            nc.scalar.copy(slot(i, S - PIECE, S), gather_flat(i, S - PIECE, S)[:])
+            if i == PACK:
+                quantise(0, 0, S)
+                for c in range(PIECES):
+                    multiply(0, c)
 
-        def gather_flat(dst, i, c):
-            window = planes[i][:].indirect(entries(offs_sb, c * PIECE, (c + 1) * PIECE))
-            nc.scalar.activation(dst, window, COPY)
-
-        pair_flat = keep.tile([P, 2, PIECE], BF16, name="pair_flat")
-        flat = keep.tile([P, PIECE], BF16, name="flat")
-        gather_into_slot(LAST - 1, 0, 3 * PIECE)
-        gather_flat(pair_flat[:, 0, :], LAST - 1, 3)
-
-        gather_into_slot(LAST, 0, HALF)
-        gather_flat(pair_flat[:, 1, :], LAST, 3)
-        gather_flat(flat[:], LAST, 2)
-        nc.scalar.copy(picked[PASSES - 1][:, 3 * PIECE :, 2:], pair_flat[:].rearrange("p t s -> p s t"))
-        nc.vector.tensor_copy(picked[PASSES - 1][:, 2 * PIECE : 3 * PIECE, PACK - 1], flat[:])
+        gather_into_slot(LAST, 0, DIRECT)
+        flat_scalar = gather_flat(LAST, S - PIECE, S)
+        flat_vector = gather_flat(LAST, DIRECT, S - PIECE)
+        nc.scalar.copy(slot(LAST, S - PIECE, S), flat_scalar[:])
+        nc.vector.tensor_copy(slot(LAST, DIRECT, S - PIECE), flat_vector[:])
         quantise(PASSES - 1, 0, HALF)
         for c in (0, 1, 3, 2):
             if c * PIECE >= HALF:
@@ -138,21 +140,28 @@ def tile_picked_sub_lin_relu_sub_e_kernel(
             else:
                 nc.scalar.activation(y[:, cols], acc[c][:, :PIECE], RELU, bias=bias[:])
 
-        halves = (slice(0, P), slice(P, V))
+        low, high = slice(0, P), slice(P, V)
         plain = [keep.tile([P, V], F32, name=f"plain{d}") for d in range(PLAIN)]
-        product = [keep.tile([P, V], F32, name=f"product{d}") for d in range(D)]
-        for d in range(PLAIN):
-            nc.scalar.activation(plain[d][:], y[:].indirect(pos_sb[d][:]), COPY)
-        for d in range(PLAIN, D):
-            nc.vector.tensor_tensor(product[d][:], y[:].indirect(pos_sb[d][:]), gate_fused[:, d - PLAIN, :], MULT)
+        fused = [keep.tile([P, V], F32, name=f"fused{j}") for j in range(D - PLAIN)]
+        first = keep.tile([P, V], F32, name="first")
+        second_low = keep.tile([P, P], F32, name="second_low")
         pair = keep.tile([P, V], F32, name="pair")
-        triple = keep.tile([P, V], F32, name="triple")
+        other = keep.tile([P, V], F32, name="other")
         total = keep.tile([P, V], F32, name="total", align_bytes=BURST)
-        nc.vector.tensor_tensor(product[0][:], plain[0][:], gate_plain[:, 0, :], MULT)
-        nc.vector.tensor_tensor(pair[:], product[2][:], product[3][:], ADD)
-        nc.vector.tensor_tensor(product[1][:], plain[1][:], gate_plain[:, 1, :], MULT)
-        for cols in halves:
-            nc.vector.tensor_tensor(triple[:, cols], pair[:, cols], product[0][:, cols], ADD)
-        for cols in halves:
-            nc.vector.tensor_tensor(total[:, cols], triple[:, cols], product[1][:, cols], ADD)
+        nc.scalar.activation(plain[0][:], y[:].indirect(pos_sb[0][:]), COPY)
+        for cols in (low, high):
+            window = y[:].indirect(entries(pos_sb[1], cols.start, cols.stop))
+            nc.scalar.activation(plain[1][:, cols], window, COPY)
+        for j in range(D - PLAIN):
+            nc.vector.tensor_tensor(fused[j][:], y[:].indirect(pos_sb[PLAIN + j][:]), gate_fused[:, j, :], MULT)
+        nc.vector.tensor_tensor(first[:], plain[0][:], gate_plain[:, 0, :], MULT)
+        nc.vector.tensor_tensor(second_low[:], plain[1][:, low], gate_plain[:, 1, low], MULT)
+        for cols in (low, high):
+            nc.vector.tensor_tensor(pair[:, cols], fused[0][:, cols], first[:, cols], ADD)
+        nc.vector.tensor_tensor(other[:, low], fused[1][:, low], second_low[:], ADD)
+        nc.vector.tensor_tensor(other[:, high], fused[1][:, high], pair[:, high], ADD)
+        second_high = plain[1][:, low]
+        nc.vector.tensor_tensor(second_high, plain[1][:, high], gate_plain[:, 1, high], MULT)
+        for cols, last in ((low, pair[:, low]), (high, second_high)):
+            nc.vector.tensor_tensor(total[:, cols], other[:, cols], last, ADD)
             nc.sync.dma_start(out[:, cols], total[:, cols])

@@ -29,7 +29,8 @@ BURST = 256
 PIECE = 128
 PIECES = S // PIECE
 HALF = S // 2
-DIRECT = 320
+CUT = 1408
+CASTS = ((0, 896, "vector"), (896, CUT, "scalar"), (CUT, 1824, "vector"), (1824, T, "scalar"))
 PLAIN = 2
 
 
@@ -58,10 +59,13 @@ def tile_picked_sub_lin_relu_sub_e_kernel(
 
         planes = [keep.tile([P, T], F32, name=f"plane{i}", align_bytes=BURST) for i in range(PLANES)]
         x_view = xT.rearrange("(a p t) w -> a t p w", a=PASSES, t=PACK)
-        for i in range(PLANES):
+        for i in range(LAST):
             nc.sync.dma_start(planes[i][:], x_view[i // PACK, i % PACK])
             if i == 0:
                 nc.sync.dma_start(offs_sb[:], offs)
+        last_view = x_view[PASSES - 1, PACK - 1]
+        nc.sync.dma_start(planes[LAST][:, :CUT], last_view[:, :CUT])
+        nc.sync.dma_start(planes[LAST][:, CUT:], last_view[:, CUT:])
         nc.sync.dma_start(w_codes[:].bitcast(I32), w_words.rearrange("a p m r -> p a (m r)").bitcast(I32))
         for q in range(4):
             nc.sync.dma_start(
@@ -79,7 +83,7 @@ def tile_picked_sub_lin_relu_sub_e_kernel(
         picked = [keep.tile([P, S, PACK], BF16, name=f"picked{a}", align_bytes=64) for a in range(PASSES)]
         x_codes = [keep.tile([P, S], U32, name=f"x_codes{a}", align_bytes=64) for a in range(PASSES)]
         x_bytes = [keep.tile([P, S], U8, name=f"x_bytes{a}", align_bytes=64) for a in range(PASSES)]
-        acc = [psum.tile([P, BANK], F32, name=f"acc{c}", tag=f"bank{c}") for c in range(PIECES)]
+        acc = [psum.tile([P, BANK], F32, name=f"acc{c}") for c in range(PIECES)]
         y = keep.tile([P, S], F32, name="y")
 
         def gather_into_slot(i, lo, hi):
@@ -123,30 +127,35 @@ def tile_picked_sub_lin_relu_sub_e_kernel(
                 for c in range(PIECES):
                     multiply(0, c)
 
-        gather_into_slot(LAST, 0, DIRECT)
-        flat_scalar = gather_flat(LAST, S - PIECE, S)
-        flat_vector = gather_flat(LAST, DIRECT, S - PIECE)
-        nc.scalar.copy(slot(LAST, S - PIECE, S), flat_scalar[:])
-        nc.vector.tensor_copy(slot(LAST, DIRECT, S - PIECE), flat_vector[:])
+        last_bf16 = keep.tile([P, T], BF16, name="last_bf16")
+        for lo, hi, engine in CASTS:
+            if engine == "vector":
+                nc.vector.tensor_copy(last_bf16[:, lo:hi], planes[LAST][:, lo:hi])
+            else:
+                nc.scalar.copy(last_bf16[:, lo:hi], planes[LAST][:, lo:hi])
+        gather_into_slot(LAST, 0, HALF)
+        nc.scalar.activation(
+            picked[PASSES - 1][:, HALF:, PACK - 1], last_bf16[:].indirect(entries(offs_sb, HALF, S)), COPY
+        )
         quantise(PASSES - 1, 0, HALF)
-        for c in (0, 1, 3, 2):
+        for c in range(PIECES):
             if c * PIECE >= HALF:
                 quantise(PASSES - 1, c * PIECE, (c + 1) * PIECE)
             multiply(PASSES - 1, c)
-        for c in (0, 1, 3, 2):
+        for c in range(PIECES):
             cols = slice(c * PIECE, (c + 1) * PIECE)
-            if c == PIECES - 1:
+            if c == PIECES - 2:
                 nc.vector.tensor_scalar(y[:, cols], acc[c][:, :PIECE], bias[:], 0.0, ADD, MAX)
             else:
                 nc.scalar.activation(y[:, cols], acc[c][:, :PIECE], RELU, bias=bias[:])
 
-        low, high = slice(0, P), slice(P, V)
+        low, high = slice(0, V // 2), slice(V // 2, V)
         plain = [keep.tile([P, V], F32, name=f"plain{d}") for d in range(PLAIN)]
         fused = [keep.tile([P, V], F32, name=f"fused{j}") for j in range(D - PLAIN)]
-        first = keep.tile([P, V], F32, name="first")
-        second_low = keep.tile([P, P], F32, name="second_low")
+        turn0 = keep.tile([P, V], F32, name="turn0")
+        turn1_low = keep.tile([P, V // 2], F32, name="turn1_low")
         pair = keep.tile([P, V], F32, name="pair")
-        other = keep.tile([P, V], F32, name="other")
+        rest = keep.tile([P, V], F32, name="rest")
         total = keep.tile([P, V], F32, name="total", align_bytes=BURST)
         nc.scalar.activation(plain[0][:], y[:].indirect(pos_sb[0][:]), COPY)
         for cols in (low, high):
@@ -154,14 +163,15 @@ def tile_picked_sub_lin_relu_sub_e_kernel(
             nc.scalar.activation(plain[1][:, cols], window, COPY)
         for j in range(D - PLAIN):
             nc.vector.tensor_tensor(fused[j][:], y[:].indirect(pos_sb[PLAIN + j][:]), gate_fused[:, j, :], MULT)
-        nc.vector.tensor_tensor(first[:], plain[0][:], gate_plain[:, 0, :], MULT)
-        nc.vector.tensor_tensor(second_low[:], plain[1][:, low], gate_plain[:, 1, low], MULT)
+
+        nc.vector.tensor_tensor(turn0[:], plain[0][:], gate_plain[:, 0, :], MULT)
+        nc.vector.tensor_tensor(turn1_low[:], plain[1][:, low], gate_plain[:, 1, low], MULT)
         for cols in (low, high):
-            nc.vector.tensor_tensor(pair[:, cols], fused[0][:, cols], first[:, cols], ADD)
-        nc.vector.tensor_tensor(other[:, low], fused[1][:, low], second_low[:], ADD)
-        nc.vector.tensor_tensor(other[:, high], fused[1][:, high], pair[:, high], ADD)
-        second_high = plain[1][:, low]
-        nc.vector.tensor_tensor(second_high, plain[1][:, high], gate_plain[:, 1, high], MULT)
-        for cols, last in ((low, pair[:, low]), (high, second_high)):
-            nc.vector.tensor_tensor(total[:, cols], other[:, cols], last, ADD)
+            nc.vector.tensor_tensor(pair[:, cols], fused[0][:, cols], turn0[:, cols], ADD)
+        nc.vector.tensor_tensor(rest[:, low], fused[1][:, low], turn1_low[:], ADD)
+        nc.vector.tensor_tensor(rest[:, high], fused[1][:, high], pair[:, high], ADD)
+        turn1_high = plain[1][:, low]
+        nc.vector.tensor_tensor(turn1_high, plain[1][:, high], gate_plain[:, 1, high], MULT)
+        for cols, addend in ((low, pair[:, low]), (high, turn1_high)):
+            nc.vector.tensor_tensor(total[:, cols], rest[:, cols], addend, ADD)
             nc.sync.dma_start(out[:, cols], total[:, cols])

@@ -31,7 +31,6 @@ PIECES = S // PIECE
 HALF = S // 2
 CUT = 1408
 CASTS = ((0, 896, "vector"), (896, CUT, "scalar"), (CUT, 1824, "vector"), (1824, T, "scalar"))
-PLAIN = 2
 
 
 def tile_picked_sub_lin_relu_sub_e_kernel(
@@ -52,8 +51,8 @@ def tile_picked_sub_lin_relu_sub_e_kernel(
         w_codes = keep.tile([P, PASSES, N], U32, name="w_codes", align_bytes=BURST)
         w_bytes = keep.tile([P, PASSES, N], U8, name="w_bytes", align_bytes=64)
         bias = keep.tile([P, 1], F32, name="bias")
-        gate_plain = keep.tile([P, PLAIN, V], F32, name="gate_plain", align_bytes=BURST)
-        gate_fused = keep.tile([P, D - PLAIN, V], F32, name="gate_fused", align_bytes=BURST)
+        gate_first = keep.tile([P, V], F32, name="gate_first", align_bytes=BURST)
+        gate_rest = keep.tile([P, D - 1, V], F32, name="gate_rest", align_bytes=BURST)
 
         nc.vector.memset(w_bytes[:].bitcast(I32), 0)
 
@@ -73,12 +72,12 @@ def tile_picked_sub_lin_relu_sub_e_kernel(
                 w_scales[:, 4 * q : 4 * q + 4, :].rearrange("a q m -> q a m").bitcast(I32),
             )
         nc.sync.dma_start(bias[:], b)
-        nc.sync.dma_start(gate_fused[:], gate[PLAIN:].rearrange("d m v -> m d v"))
-        nc.sync.dma_start(pos_sb[2][:], pos3)
-        nc.sync.dma_start(pos_sb[0][:], pos1)
+        nc.sync.dma_start(gate_first[:], gate[D - 1])
         nc.sync.dma_start(pos_sb[3][:], pos4)
+        nc.sync.dma_start(pos_sb[0][:], pos1)
+        nc.sync.dma_start(pos_sb[2][:], pos3)
         nc.sync.dma_start(pos_sb[1][:], pos2)
-        nc.sync.dma_start(gate_plain[:], gate[:PLAIN].rearrange("d m v -> m d v"))
+        nc.sync.dma_start(gate_rest[:], gate[: D - 1].rearrange("d m v -> m d v"))
 
         picked = [keep.tile([P, S, PACK], BF16, name=f"picked{a}", align_bytes=64) for a in range(PASSES)]
         x_codes = [keep.tile([P, S], U32, name=f"x_codes{a}", align_bytes=64) for a in range(PASSES)]
@@ -149,29 +148,34 @@ def tile_picked_sub_lin_relu_sub_e_kernel(
             else:
                 nc.scalar.activation(y[:, cols], acc[c][:, :PIECE], RELU, bias=bias[:])
 
-        low, high = slice(0, V // 2), slice(V // 2, V)
-        plain = [keep.tile([P, V], F32, name=f"plain{d}") for d in range(PLAIN)]
-        fused = [keep.tile([P, V], F32, name=f"fused{j}") for j in range(D - PLAIN)]
-        turn0 = keep.tile([P, V], F32, name="turn0")
-        turn1_low = keep.tile([P, V // 2], F32, name="turn1_low")
-        pair = keep.tile([P, V], F32, name="pair")
-        rest = keep.tile([P, V], F32, name="rest")
+        low, high, whole = slice(0, V // 2), slice(V // 2, V), slice(0, V)
+        plain = [keep.tile([P, V], F32, name=f"plain{d}") for d in range(D - 1)]
+        term = [keep.tile([P, V], F32, name=f"term{d}") for d in range(D)]
+        two = keep.tile([P, V], F32, name="two")
+        three = keep.tile([P, V], F32, name="three")
         total = keep.tile([P, V], F32, name="total", align_bytes=BURST)
-        nc.scalar.activation(plain[0][:], y[:].indirect(pos_sb[0][:]), COPY)
-        for cols in (low, high):
-            window = y[:].indirect(entries(pos_sb[1], cols.start, cols.stop))
-            nc.scalar.activation(plain[1][:, cols], window, COPY)
-        for j in range(D - PLAIN):
-            nc.vector.tensor_tensor(fused[j][:], y[:].indirect(pos_sb[PLAIN + j][:]), gate_fused[:, j, :], MULT)
 
-        nc.vector.tensor_tensor(turn0[:], plain[0][:], gate_plain[:, 0, :], MULT)
-        nc.vector.tensor_tensor(turn1_low[:], plain[1][:, low], gate_plain[:, 1, low], MULT)
+        def window(d, cols):
+            return y[:].indirect(entries(pos_sb[d], cols.start, cols.stop))
+
+        def weigh(d, cols):
+            nc.vector.tensor_tensor(term[d][:, cols], plain[d][:, cols], gate_rest[:, d, cols], MULT)
+
+        def add(result, cols, left, right):
+            nc.vector.tensor_tensor(result[:, cols], left[:, cols], right[:, cols], ADD)
+
+        for d, cols in ((0, whole), (2, high), (1, low), (1, high)):
+            nc.scalar.activation(plain[d][:, cols], window(d, cols), COPY)
+        nc.vector.tensor_tensor(term[3][:], window(3, whole), gate_first[:], MULT)
+        nc.vector.tensor_tensor(term[2][:, low], window(2, low), gate_rest[:, 2, low], MULT)
+        weigh(0, whole)
+        add(two, low, term[3], term[2])
+        weigh(2, high)
+        add(two, high, term[3], term[0])
+        add(three, low, two, term[0])
+        weigh(1, low)
+        add(three, high, two, term[2])
+        weigh(1, high)
         for cols in (low, high):
-            nc.vector.tensor_tensor(pair[:, cols], fused[0][:, cols], turn0[:, cols], ADD)
-        nc.vector.tensor_tensor(rest[:, low], fused[1][:, low], turn1_low[:], ADD)
-        nc.vector.tensor_tensor(rest[:, high], fused[1][:, high], pair[:, high], ADD)
-        turn1_high = plain[1][:, low]
-        nc.vector.tensor_tensor(turn1_high, plain[1][:, high], gate_plain[:, 1, high], MULT)
-        for cols, addend in ((low, pair[:, low]), (high, turn1_high)):
-            nc.vector.tensor_tensor(total[:, cols], rest[:, cols], addend, ADD)
+            add(total, cols, three, term[1])
             nc.sync.dma_start(out[:, cols], total[:, cols])

@@ -29,8 +29,8 @@ BURST = 256
 PIECE = 128
 PIECES = S // PIECE
 HALF = S // 2
-CUT = 1408
-CASTS = ((0, 896, "vector"), (896, CUT, "scalar"), (CUT, 1824, "vector"), (1824, T, "scalar"))
+CUTS = (0, 1280, 1792, T)
+SHARES = (832, 1600, 1920)
 
 
 def tile_picked_sub_lin_relu_sub_e_kernel(
@@ -56,15 +56,17 @@ def tile_picked_sub_lin_relu_sub_e_kernel(
 
         nc.vector.memset(w_bytes[:].bitcast(I32), 0)
 
-        planes = [keep.tile([P, T], F32, name=f"plane{i}", align_bytes=BURST) for i in range(PLANES)]
+        first_two = keep.tile([P, 2, T], F32, name="first_two", align_bytes=BURST)
+        planes = [first_two[:, 0, :], first_two[:, 1, :]]
+        planes.extend(keep.tile([P, T], F32, name=f"plane{i}", align_bytes=BURST) for i in range(2, PLANES))
         x_view = xT.rearrange("(a p t) w -> a t p w", a=PASSES, t=PACK)
-        for i in range(LAST):
+        nc.sync.dma_start(first_two[:], xT.rearrange("(a p t) w -> a p t w", a=PASSES, t=PACK)[0, :, 0:2, :])
+        nc.sync.dma_start(offs_sb[:], offs)
+        for i in range(2, LAST):
             nc.sync.dma_start(planes[i][:], x_view[i // PACK, i % PACK])
-            if i == 0:
-                nc.sync.dma_start(offs_sb[:], offs)
         last_view = x_view[PASSES - 1, PACK - 1]
-        nc.sync.dma_start(planes[LAST][:, :CUT], last_view[:, :CUT])
-        nc.sync.dma_start(planes[LAST][:, CUT:], last_view[:, CUT:])
+        for lo, hi in zip(CUTS, CUTS[1:]):
+            nc.sync.dma_start(planes[LAST][:, lo:hi], last_view[:, lo:hi])
         nc.sync.dma_start(w_codes[:].bitcast(I32), w_words.rearrange("a p m r -> p a (m r)").bitcast(I32))
         for q in range(4):
             nc.sync.dma_start(
@@ -127,19 +129,15 @@ def tile_picked_sub_lin_relu_sub_e_kernel(
                     multiply(0, c)
 
         last_bf16 = keep.tile([P, T], BF16, name="last_bf16")
-        for lo, hi, engine in CASTS:
-            if engine == "vector":
-                nc.vector.tensor_copy(last_bf16[:, lo:hi], planes[LAST][:, lo:hi])
-            else:
-                nc.scalar.copy(last_bf16[:, lo:hi], planes[LAST][:, lo:hi])
+        for lo, mid, hi in zip(CUTS, SHARES, CUTS[1:]):
+            nc.vector.tensor_copy(last_bf16[:, lo:mid], planes[LAST][:, lo:mid])
+            nc.scalar.copy(last_bf16[:, mid:hi], planes[LAST][:, mid:hi])
         gather_into_slot(LAST, 0, HALF)
         nc.scalar.activation(
             picked[PASSES - 1][:, HALF:, PACK - 1], last_bf16[:].indirect(entries(offs_sb, HALF, S)), COPY
         )
-        quantise(PASSES - 1, 0, HALF)
         for c in range(PIECES):
-            if c * PIECE >= HALF:
-                quantise(PASSES - 1, c * PIECE, (c + 1) * PIECE)
+            quantise(PASSES - 1, c * PIECE, (c + 1) * PIECE)
             multiply(PASSES - 1, c)
         for c in range(PIECES):
             cols = slice(c * PIECE, (c + 1) * PIECE)

@@ -56,23 +56,28 @@ def tile_picked_sub_lin_relu_sub_e_kernel(
 
         nc.vector.memset(w_bytes[:].bitcast(I32), 0)
 
-        first_two = keep.tile([P, 2, T], F32, name="first_two", align_bytes=BURST)
-        planes = [first_two[:, 0, :], first_two[:, 1, :]]
-        planes.extend(keep.tile([P, T], F32, name=f"plane{i}", align_bytes=BURST) for i in range(2, PLANES))
+        pairs = [keep.tile([P, 2, T], F32, name=f"pair{u}", align_bytes=BURST) for u in range(PACK // 2)]
+        planes = [pairs[i // 2][:, i % 2, :] for i in range(PACK)]
+        planes.extend(keep.tile([P, T], F32, name=f"plane{i}", align_bytes=BURST) for i in range(PACK, PLANES))
         x_view = xT.rearrange("(a p t) w -> a t p w", a=PASSES, t=PACK)
-        nc.sync.dma_start(first_two[:], xT.rearrange("(a p t) w -> a p t w", a=PASSES, t=PACK)[0, :, 0:2, :])
-        nc.sync.dma_start(offs_sb[:], offs)
-        for i in range(2, LAST):
+        pair_view = xT.rearrange("(a p u e) w -> a u p e w", a=PASSES, u=PACK // 2, e=2)
+        for u in range(PACK // 2):
+            nc.sync.dma_start(pairs[u][:], pair_view[0, u])
+            if u == 0:
+                nc.sync.dma_start(offs_sb[:], offs)
+        for i in range(PACK, LAST):
             nc.sync.dma_start(planes[i][:], x_view[i // PACK, i % PACK])
         last_view = x_view[PASSES - 1, PACK - 1]
         for lo, hi in zip(CUTS, CUTS[1:]):
             nc.sync.dma_start(planes[LAST][:, lo:hi], last_view[:, lo:hi])
-        nc.sync.dma_start(w_codes[:].bitcast(I32), w_words.rearrange("a p m r -> p a (m r)").bitcast(I32))
+        w_view = w_words.rearrange("a p m r -> a p (m r)").bitcast(I32)
+        nc.sync.dma_start(w_codes[:, 0, :].bitcast(I32), w_view[0])
         for q in range(4):
             nc.sync.dma_start(
                 w_bytes[32 * q : 32 * q + 4].bitcast(I32),
                 w_scales[:, 4 * q : 4 * q + 4, :].rearrange("a q m -> q a m").bitcast(I32),
             )
+        nc.sync.dma_start(w_codes[:, 1, :].bitcast(I32), w_view[1])
         nc.sync.dma_start(bias[:], b)
         nc.sync.dma_start(gate_first[:], gate[D - 1])
         nc.sync.dma_start(pos_sb[3][:], pos4)
@@ -111,16 +116,16 @@ def tile_picked_sub_lin_relu_sub_e_kernel(
             )
 
         def gather_flat(i, lo, hi):
-            flat = keep.tile([P, hi - lo], BF16, name=f"flat{i}_{lo}")
+            flat = keep.tile([P, hi - lo], BF16 if i >= PACK else F32, name=f"flat{i}_{lo}")
             nc.scalar.activation(flat[:], planes[i][:].indirect(entries(offs_sb, lo, hi)), COPY)
             return flat
 
         def slot(i, lo, hi):
             return picked[i // PACK][:, lo:hi, i % PACK]
 
-        for i in range(PACK):
+        for i in range(PACK // 2):
             gather_into_slot(i, 0, S)
-        for i in range(PACK, LAST):
+        for i in range(PACK // 2, LAST):
             gather_into_slot(i, 0, S - PIECE)
             nc.scalar.copy(slot(i, S - PIECE, S), gather_flat(i, S - PIECE, S)[:])
             if i == PACK:
@@ -173,7 +178,11 @@ def tile_picked_sub_lin_relu_sub_e_kernel(
         add(three, low, two, term[0])
         weigh(1, low)
         add(three, high, two, term[2])
-        weigh(1, high)
-        for cols in (low, high):
+        quarters = (slice(V // 2, 3 * V // 4), slice(3 * V // 4, V))
+        for cols in quarters:
+            weigh(1, cols)
+        add(total, low, three, term[1])
+        nc.sync.dma_start(out[:, low], total[:, low])
+        for cols in quarters:
             add(total, cols, three, term[1])
-            nc.sync.dma_start(out[:, cols], total[:, cols])
+        nc.sync.dma_start(out[:, high], total[:, high])

@@ -29,8 +29,6 @@ BURST = 256
 PIECE = 128
 PIECES = S // PIECE
 HALF = S // 2
-CUTS = (0, 1280, 1792, T)
-SHARES = (832, 1600, 1920)
 
 
 def tile_picked_sub_lin_relu_sub_e_kernel(
@@ -65,11 +63,8 @@ def tile_picked_sub_lin_relu_sub_e_kernel(
             nc.sync.dma_start(pairs[u][:], pair_view[0, u])
             if u == 0:
                 nc.sync.dma_start(offs_sb[:], offs)
-        for i in range(PACK, LAST):
+        for i in range(PACK, PLANES):
             nc.sync.dma_start(planes[i][:], x_view[i // PACK, i % PACK])
-        last_view = x_view[PASSES - 1, PACK - 1]
-        for lo, hi in zip(CUTS, CUTS[1:]):
-            nc.sync.dma_start(planes[LAST][:, lo:hi], last_view[:, lo:hi])
         w_view = w_words.rearrange("a p m r -> a p (m r)").bitcast(I32)
         nc.sync.dma_start(w_codes[:, 0, :].bitcast(I32), w_view[0])
         for q in range(4):
@@ -116,7 +111,7 @@ def tile_picked_sub_lin_relu_sub_e_kernel(
             )
 
         def gather_flat(i, lo, hi):
-            flat = keep.tile([P, hi - lo], BF16 if i >= PACK else F32, name=f"flat{i}_{lo}")
+            flat = keep.tile([P, hi - lo], F32, name=f"flat{i}_{lo}")
             nc.scalar.activation(flat[:], planes[i][:].indirect(entries(offs_sb, lo, hi)), COPY)
             return flat
 
@@ -126,21 +121,20 @@ def tile_picked_sub_lin_relu_sub_e_kernel(
         for i in range(PACK // 2):
             gather_into_slot(i, 0, S)
         for i in range(PACK // 2, LAST):
-            gather_into_slot(i, 0, S - PIECE)
-            nc.scalar.copy(slot(i, S - PIECE, S), gather_flat(i, S - PIECE, S)[:])
+            cut = S - PIECE if i < LAST - 1 else S - 64
+            gather_into_slot(i, 0, cut)
+            nc.scalar.copy(slot(i, cut, S), gather_flat(i, cut, S)[:])
             if i == PACK:
                 quantise(0, 0, S)
                 for c in range(PIECES):
                     multiply(0, c)
 
-        last_bf16 = keep.tile([P, T], BF16, name="last_bf16")
-        for lo, mid, hi in zip(CUTS, SHARES, CUTS[1:]):
-            nc.vector.tensor_copy(last_bf16[:, lo:mid], planes[LAST][:, lo:mid])
-            nc.scalar.copy(last_bf16[:, mid:hi], planes[LAST][:, mid:hi])
-        gather_into_slot(LAST, 0, HALF)
-        nc.scalar.activation(
-            picked[PASSES - 1][:, HALF:, PACK - 1], last_bf16[:].indirect(entries(offs_sb, HALF, S)), COPY
-        )
+        stepped, own = 320, S - 64
+        gather_into_slot(LAST, 0, stepped)
+        given = gather_flat(LAST, stepped, own)
+        kept = gather_flat(LAST, own, S)
+        nc.vector.tensor_copy(slot(LAST, stepped, own), given[:])
+        nc.scalar.copy(slot(LAST, own, S), kept[:])
         for c in range(PIECES):
             quantise(PASSES - 1, c * PIECE, (c + 1) * PIECE)
             multiply(PASSES - 1, c)

@@ -54,17 +54,12 @@ def tile_picked_sub_lin_relu_sub_e_kernel(
 
         nc.vector.memset(w_bytes[:].bitcast(I32), 0)
 
-        pairs = [keep.tile([P, 2, T], F32, name=f"pair{u}", align_bytes=BURST) for u in range(PACK // 2)]
-        planes = [pairs[i // 2][:, i % 2, :] for i in range(PACK)]
-        planes.extend(keep.tile([P, T], F32, name=f"plane{i}", align_bytes=BURST) for i in range(PACK, PLANES))
+        planes = [keep.tile([P, T], F32, name=f"plane{i}", align_bytes=BURST) for i in range(PLANES)]
         x_view = xT.rearrange("(a p t) w -> a t p w", a=PASSES, t=PACK)
-        pair_view = xT.rearrange("(a p u e) w -> a u p e w", a=PASSES, u=PACK // 2, e=2)
-        for u in range(PACK // 2):
-            nc.sync.dma_start(pairs[u][:], pair_view[0, u])
-            if u == 0:
-                nc.sync.dma_start(offs_sb[:], offs)
-        for i in range(PACK, PLANES):
+        for i in range(PLANES):
             nc.sync.dma_start(planes[i][:], x_view[i // PACK, i % PACK])
+            if i == 0:
+                nc.sync.dma_start(offs_sb[:], offs)
         w_view = w_words.rearrange("a p m r -> a p (m r)").bitcast(I32)
         nc.sync.dma_start(w_codes[:, 0, :].bitcast(I32), w_view[0])
         for q in range(4):
@@ -118,10 +113,10 @@ def tile_picked_sub_lin_relu_sub_e_kernel(
         def slot(i, lo, hi):
             return picked[i // PACK][:, lo:hi, i % PACK]
 
-        for i in range(PACK // 2):
+        for i in range(PACK):
             gather_into_slot(i, 0, S)
-        for i in range(PACK // 2, LAST):
-            cut = S - PIECE if i < LAST - 1 else S - 64
+        for i in range(PACK, LAST):
+            cut = S - PIECE if i < LAST - 1 else S - 96
             gather_into_slot(i, 0, cut)
             nc.scalar.copy(slot(i, cut, S), gather_flat(i, cut, S)[:])
             if i == PACK:
@@ -129,7 +124,7 @@ def tile_picked_sub_lin_relu_sub_e_kernel(
                 for c in range(PIECES):
                     multiply(0, c)
 
-        stepped, own = 320, S - 64
+        stepped, own = 288, S - 96
         gather_into_slot(LAST, 0, stepped)
         given = gather_flat(LAST, stepped, own)
         kept = gather_flat(LAST, own, S)

@@ -54,12 +54,17 @@ def tile_picked_sub_lin_relu_sub_e_kernel(
 
         nc.vector.memset(w_bytes[:].bitcast(I32), 0)
 
-        planes = [keep.tile([P, T], F32, name=f"plane{i}", align_bytes=BURST) for i in range(PLANES)]
+        pairs = [keep.tile([P, 2, T], F32, name=f"pair{u}", align_bytes=BURST) for u in range(PACK // 2)]
+        planes = [pairs[i // 2][:, i % 2, :] for i in range(PACK)]
+        planes.extend(keep.tile([P, T], F32, name=f"plane{i}", align_bytes=BURST) for i in range(PACK, PLANES))
         x_view = xT.rearrange("(a p t) w -> a t p w", a=PASSES, t=PACK)
-        for i in range(PLANES):
-            nc.sync.dma_start(planes[i][:], x_view[i // PACK, i % PACK])
-            if i == 0:
+        pair_view = xT.rearrange("(a p u e) w -> a u p e w", a=PASSES, u=PACK // 2, e=2)
+        for u in range(PACK // 2):
+            nc.sync.dma_start(pairs[u][:], pair_view[0, u])
+            if u == 0:
                 nc.sync.dma_start(offs_sb[:], offs)
+        for i in range(PACK, PLANES):
+            nc.sync.dma_start(planes[i][:], x_view[i // PACK, i % PACK])
         w_view = w_words.rearrange("a p m r -> a p (m r)").bitcast(I32)
         nc.sync.dma_start(w_codes[:, 0, :].bitcast(I32), w_view[0])
         for q in range(4):
@@ -113,9 +118,9 @@ def tile_picked_sub_lin_relu_sub_e_kernel(
         def slot(i, lo, hi):
             return picked[i // PACK][:, lo:hi, i % PACK]
 
-        for i in range(PACK):
+        for i in range(PACK // 2):
             gather_into_slot(i, 0, S)
-        for i in range(PACK, LAST):
+        for i in range(PACK // 2, LAST):
             cut = S - PIECE if i < LAST - 1 else S - 96
             gather_into_slot(i, 0, cut)
             nc.scalar.copy(slot(i, cut, S), gather_flat(i, cut, S)[:])

@@ -76,8 +76,8 @@ def tile_picked_sub_lin_relu_sub_e_kernel(
         nc.sync.dma_start(bias[:], b)
         nc.sync.dma_start(gate_first[:], gate[D - 1])
         nc.sync.dma_start(pos_sb[3][:], pos4)
-        nc.sync.dma_start(pos_sb[0][:], pos1)
         nc.sync.dma_start(pos_sb[2][:], pos3)
+        nc.sync.dma_start(pos_sb[0][:], pos1)
         nc.sync.dma_start(pos_sb[1][:], pos2)
         nc.sync.dma_start(gate_rest[:], gate[: D - 1].rearrange("d m v -> m d v"))
 
@@ -161,17 +161,18 @@ def tile_picked_sub_lin_relu_sub_e_kernel(
         def add(result, cols, left, right):
             nc.vector.tensor_tensor(result[:, cols], left[:, cols], right[:, cols], ADD)
 
-        for d, cols in ((0, whole), (2, high), (1, low), (1, high)):
+        for d, cols in ((2, high), (0, low), (0, high), (1, low), (1, high)):
             nc.scalar.activation(plain[d][:, cols], window(d, cols), COPY)
         nc.vector.tensor_tensor(term[3][:], window(3, whole), gate_first[:], MULT)
         nc.vector.tensor_tensor(term[2][:, low], window(2, low), gate_rest[:, 2, low], MULT)
-        weigh(0, whole)
-        add(two, low, term[3], term[2])
         weigh(2, high)
-        add(two, high, term[3], term[0])
+        add(two, low, term[3], term[2])
+        weigh(0, low)
+        add(two, high, term[3], term[2])
+        weigh(0, high)
         add(three, low, two, term[0])
         weigh(1, low)
-        add(three, high, two, term[2])
+        add(three, high, two, term[0])
         quarters = (slice(V // 2, 3 * V // 4), slice(3 * V // 4, V))
         for cols in quarters:
             weigh(1, cols)

@@ -59,10 +59,10 @@ def tile_picked_sub_lin_relu_sub_e_kernel(
         planes.extend(keep.tile([P, T], F32, name=f"plane{i}", align_bytes=BURST) for i in range(PACK, PLANES))
         x_view = xT.rearrange("(a p t) w -> a t p w", a=PASSES, t=PACK)
         pair_view = xT.rearrange("(a p u e) w -> a u p e w", a=PASSES, u=PACK // 2, e=2)
-        for u in range(PACK // 2):
-            nc.sync.dma_start(pairs[u][:], pair_view[0, u])
-            if u == 0:
-                nc.sync.dma_start(offs_sb[:], offs)
+        nc.scalar.dma_start(planes[0], x_view[0, 0])
+        nc.sync.dma_start(offs_sb[:], offs)
+        nc.sync.dma_start(planes[1], x_view[0, 1])
+        nc.sync.dma_start(pairs[1][:], pair_view[0, 1])
         for i in range(PACK, PLANES):
             nc.sync.dma_start(planes[i][:], x_view[i // PACK, i % PACK])
         w_view = w_words.rearrange("a p m r -> a p (m r)").bitcast(I32)

@@ -178,6 +178,6 @@ def tile_picked_sub_lin_relu_sub_e_kernel(
             weigh(1, cols)
         add(total, low, three, term[1])
         nc.sync.dma_start(out[:, low], total[:, low])
-        for cols in quarters:
+        for cols, queue in zip(quarters, (nc.scalar, nc.sync)):
             add(total, cols, three, term[1])
-        nc.sync.dma_start(out[:, high], total[:, high])
+            queue.dma_start(out[:, cols], total[:, cols])

@@ -59,9 +59,9 @@ def tile_picked_sub_lin_relu_sub_e_kernel(
         planes.extend(keep.tile([P, T], F32, name=f"plane{i}", align_bytes=BURST) for i in range(PACK, PLANES))
         x_view = xT.rearrange("(a p t) w -> a t p w", a=PASSES, t=PACK)
         pair_view = xT.rearrange("(a p u e) w -> a u p e w", a=PASSES, u=PACK // 2, e=2)
-        nc.scalar.dma_start(planes[0], x_view[0, 0])
+        nc.sync.dma_start(planes[0], x_view[0, 0])
+        nc.scalar.dma_start(planes[1], x_view[0, 1])
         nc.sync.dma_start(offs_sb[:], offs)
-        nc.sync.dma_start(planes[1], x_view[0, 1])
         nc.sync.dma_start(pairs[1][:], pair_view[0, 1])
         for i in range(PACK, PLANES):
             nc.sync.dma_start(planes[i][:], x_view[i // PACK, i % PACK])

from contextlib import ExitStack

import concourse.mybir as mybir

K, T, D, S, V, N = 1024, 2048, 4, 512, 256, 128
FLOPS = 2 * K * N * S

F32 = mybir.dt.float32
BF16 = mybir.dt.bfloat16
I32 = mybir.dt.int32
U32 = mybir.dt.uint32
U16 = mybir.dt.uint16
U8 = mybir.dt.uint8
FP8X4 = mybir.dt.float8_e4m3fn_x4
ADD = mybir.AluOpType.add
MULT = mybir.AluOpType.mult
MAX = mybir.AluOpType.max
COPY = mybir.ActivationFunctionType.Copy
RELU = mybir.ActivationFunctionType.Relu

P = 128
PACK = 4
PASSES = K // (P * PACK)
PLANES = PASSES * PACK
LAST = PLANES - 1
PER_COLUMN = 16
BANK = 512
BURST = 256
PIECE = 128
PIECES = S // PIECE
HALF = S // 2


def tile_picked_sub_lin_relu_sub_e_kernel(
    tc, xT, w_words, w_scales, b, gate, offs, pos1, pos2, pos3, pos4, out
):
    nc = tc.nc
    with ExitStack() as ctx:
        lists = ctx.enter_context(tc.tile_pool(name="lists", bufs=1))
        keep = ctx.enter_context(tc.tile_pool(name="keep", bufs=1))
        psum = ctx.enter_context(tc.psum_pool(name="psum", bufs=1))

        offs_sb = lists.tile([P, S // PER_COLUMN], U16, name="offs_sb")
        pos_sb = [lists.tile([P, V // PER_COLUMN], U16, name=f"pos_sb{d}") for d in range(D)]

        def entries(list_sb, lo, hi):
            return list_sb[:, lo // PER_COLUMN : hi // PER_COLUMN]

        w_codes = keep.tile([P, PASSES, N], U32, name="w_codes", align_bytes=BURST)
        w_bytes = keep.tile([P, PASSES, N], U8, name="w_bytes", align_bytes=64)
        bias = keep.tile([P, 1], F32, name="bias")
        gate_first = keep.tile([P, V], F32, name="gate_first", align_bytes=BURST)
        gate_rest = keep.tile([P, D - 1, V], F32, name="gate_rest", align_bytes=BURST)

        nc.vector.memset(w_bytes[:].bitcast(I32), 0)

        pairs = [keep.tile([P, 2, T], F32, name=f"pair{u}", align_bytes=BURST) for u in range(PACK // 2)]
        planes = [pairs[i // 2][:, i % 2, :] for i in range(PACK)]
        planes.extend(keep.tile([P, T], F32, name=f"plane{i}", align_bytes=BURST) for i in range(PACK, PLANES))
        x_view = xT.rearrange("(a p t) w -> a t p w", a=PASSES, t=PACK)
        pair_view = xT.rearrange("(a p u e) w -> a u p e w", a=PASSES, u=PACK // 2, e=2)
        nc.sync.dma_start(planes[0], x_view[0, 0])
        nc.scalar.dma_start(planes[1], x_view[0, 1])
        nc.sync.dma_start(offs_sb[:], offs)
        nc.sync.dma_start(pairs[1][:], pair_view[0, 1])
        for i in range(PACK, PLANES):
            nc.sync.dma_start(planes[i][:], x_view[i // PACK, i % PACK])
        w_view = w_words.rearrange("a p m r -> a p (m r)").bitcast(I32)
        nc.sync.dma_start(w_codes[:, 0, :].bitcast(I32), w_view[0])
        for q in range(4):
            nc.sync.dma_start(
                w_bytes[32 * q : 32 * q + 4].bitcast(I32),
                w_scales[:, 4 * q : 4 * q + 4, :].rearrange("a q m -> q a m").bitcast(I32),
            )
        nc.sync.dma_start(w_codes[:, 1, :].bitcast(I32), w_view[1])
        nc.sync.dma_start(bias[:], b)
        nc.sync.dma_start(gate_first[:], gate[D - 1])
        nc.sync.dma_start(pos_sb[3][:], pos4)
        nc.sync.dma_start(pos_sb[2][:], pos3)
        nc.sync.dma_start(pos_sb[0][:], pos1)
        nc.sync.dma_start(pos_sb[1][:], pos2)
        nc.sync.dma_start(gate_rest[:], gate[: D - 1].rearrange("d m v -> m d v"))

        picked = [keep.tile([P, S, PACK], BF16, name=f"picked{a}", align_bytes=64) for a in range(PASSES)]
        x_codes = [keep.tile([P, S], U32, name=f"x_codes{a}", align_bytes=64) for a in range(PASSES)]
        x_bytes = [keep.tile([P, S], U8, name=f"x_bytes{a}", align_bytes=64) for a in range(PASSES)]
        acc = [psum.tile([P, BANK], F32, name=f"acc{c}") for c in range(PIECES)]
        y = keep.tile([P, S], F32, name="y")

        def gather_into_slot(i, lo, hi):
            window = planes[i][:].indirect(entries(offs_sb, lo, hi))
            nc.vector.tensor_copy(picked[i // PACK][:, lo:hi, i % PACK], window)

        def quantise(a, lo, hi):
            nc.vector.quantize_mx(
                out=x_codes[a][:, lo:hi].bitcast(FP8X4),
                scales=x_bytes[a][:, lo:hi],
                in_=picked[a][:, lo:hi, :].rearrange("p s t -> p (s t)"),
            )

        def multiply(a, c):
            cols = slice(c * PIECE, (c + 1) * PIECE)
            nc.tensor.matmul_mx(
                out=acc[c][:, :PIECE],
                lhsT=w_codes[:, a, :].bitcast(FP8X4),
                lhsT_scale=w_bytes[:, a, :],
                rhs=x_codes[a][:, cols].bitcast(FP8X4),
                rhs_scale=x_bytes[a][:, cols],
                start=(a == 0),
                stop=(a == PASSES - 1),
            )

        def gather_flat(i, lo, hi):
            flat = keep.tile([P, hi - lo], F32, name=f"flat{i}_{lo}")
            nc.scalar.activation(flat[:], planes[i][:].indirect(entries(offs_sb, lo, hi)), COPY)
            return flat

        def slot(i, lo, hi):
            return picked[i // PACK][:, lo:hi, i % PACK]

        for i in range(PACK // 2):
            gather_into_slot(i, 0, S)
        for i in range(PACK // 2, LAST):
            cut = S - PIECE if i < LAST - 1 else S - 96
            gather_into_slot(i, 0, cut)
            nc.scalar.copy(slot(i, cut, S), gather_flat(i, cut, S)[:])
            if i == PACK:
                quantise(0, 0, S)
                for c in range(PIECES):
                    multiply(0, c)

        stepped, own = 288, S - 96
        gather_into_slot(LAST, 0, stepped)
        given = gather_flat(LAST, stepped, own)
        kept = gather_flat(LAST, own, S)
        nc.vector.tensor_copy(slot(LAST, stepped, own), given[:])
        nc.scalar.copy(slot(LAST, own, S), kept[:])
        for c in range(PIECES):
            quantise(PASSES - 1, c * PIECE, (c + 1) * PIECE)
            multiply(PASSES - 1, c)
        for c in range(PIECES):
            cols = slice(c * PIECE, (c + 1) * PIECE)
            if c == PIECES - 2:
                nc.vector.tensor_scalar(y[:, cols], acc[c][:, :PIECE], bias[:], 0.0, ADD, MAX)
            else:
                nc.scalar.activation(y[:, cols], acc[c][:, :PIECE], RELU, bias=bias[:])

        low, high, whole = slice(0, V // 2), slice(V // 2, V), slice(0, V)
        plain = [keep.tile([P, V], F32, name=f"plain{d}") for d in range(D - 1)]
        term = [keep.tile([P, V], F32, name=f"term{d}") for d in range(D)]
        two = keep.tile([P, V], F32, name="two")
        three = keep.tile([P, V], F32, name="three")
        total = keep.tile([P, V], F32, name="total", align_bytes=BURST)

        def window(d, cols):
            return y[:].indirect(entries(pos_sb[d], cols.start, cols.stop))

        def weigh(d, cols):
            nc.vector.tensor_tensor(term[d][:, cols], plain[d][:, cols], gate_rest[:, d, cols], MULT)

        def add(result, cols, left, right):
            nc.vector.tensor_tensor(result[:, cols], left[:, cols], right[:, cols], ADD)

        for d, cols in ((2, high), (0, low), (0, high), (1, low), (1, high)):
            nc.scalar.activation(plain[d][:, cols], window(d, cols), COPY)
        nc.vector.tensor_tensor(term[3][:], window(3, whole), gate_first[:], MULT)
        nc.vector.tensor_tensor(term[2][:, low], window(2, low), gate_rest[:, 2, low], MULT)
        weigh(2, high)
        add(two, low, term[3], term[2])
        weigh(0, low)
        add(two, high, term[3], term[2])
        weigh(0, high)
        add(three, low, two, term[0])
        weigh(1, low)
        add(three, high, two, term[0])
        quarters = (slice(V // 2, 3 * V // 4), slice(3 * V // 4, V))
        for cols in quarters:
            weigh(1, cols)
        add(total, low, three, term[1])
        nc.sync.dma_start(out[:, low], total[:, low])
        for cols, queue in zip(quarters, (nc.scalar, nc.sync)):
            add(total, cols, three, term[1])
            queue.dma_start(out[:, cols], total[:, cols])
